import numpy as np
import ml_dtypes


def mxq(x, axis, fmt="e4m3"):
    dtype, down = {"e4m3": (ml_dtypes.float8_e4m3fn, 7), "e5m2": (ml_dtypes.float8_e5m2, 14)}[fmt]
    v = np.moveaxis(np.asarray(x, np.float32).astype(ml_dtypes.bfloat16).astype(np.float64), axis, -1)
    blocks = v.reshape(v.shape[:-1] + (-1, 32))
    amax = np.abs(blocks).max(-1, keepdims=True)
    byte = np.maximum(np.where(amax > 0, np.frexp(amax)[1] - 1 + 127, 0) - down, 1)
    scale = np.exp2(byte - 127.0)
    codes = (blocks / scale).astype(np.float32).astype(dtype).astype(np.float64)
    return np.moveaxis((codes * scale).reshape(v.shape), -1, axis)


WIDE = False


def mx_kscale(k):
    if not WIDE:
        return np.ones(k)
    levels = np.array([10, -10, 5, -5, 0])
    if k % 512:
        return np.exp2(np.random.permutation(np.resize(levels, k // 32))).repeat(32)
    a = np.empty((k // 512, 16))
    for p in range(k // 512):
        a[p, :8] = np.random.permutation(np.resize(levels, 8))
        for g in range(8):
            far = levels[np.abs(levels - a[p, g]) >= 10]
            a[p, g + 8] = far[np.random.randint(len(far))]
    return np.exp2(a.ravel()).repeat(32)


BF16 = ml_dtypes.bfloat16


def bf(x):
    return np.asarray(x, np.float32).astype(BF16)


def f64(x):
    return np.asarray(x).astype(np.float64)


M, K, F, N, J = 1024, 1536, 512, 2048, 1024


def draw0():
    s, r, t, u = mx_kscale(K), mx_kscale(J), mx_kscale(F), mx_kscale(M)
    return {"x": bf(np.random.standard_normal((M, K)) * s),
            "w_q": bf(np.random.standard_normal((K, F)) / np.sqrt(K) / s[:, None]),
            "b_q": bf(0.3 * np.random.standard_normal(F)),
            "gain": bf((1 + 0.1 * np.random.standard_normal(F)) * t),
            "conf": bf(np.exp(0.2 * np.random.standard_normal(M)) * u),
            "y": bf(np.random.standard_normal((N, J)) * r),
            "w_d": bf(np.random.standard_normal((J, F)) / np.sqrt(J) / r[:, None] / t),
            "b_d": bf(0.3 * np.random.standard_normal(F) / t),
            "inv_temp": bf(np.exp(0.2 * np.random.standard_normal(M)) / np.sqrt(F) / u),
            "prior": bf(0.3 * np.random.standard_normal(N)),
            "clicks": bf(np.random.standard_normal((N, M)) / np.sqrt(M) / u),
            "keep": bf((1 + 0.1 * np.random.standard_normal(F)) * t),
            "move": bf((1 + 0.1 * np.random.standard_normal(F)) / t)}


def core(x, w_q, b_q, gain, conf, y, w_d, b_d, inv_temp, prior, clicks, keep, move):
    v = (mxq(f64(x), 1, "e4m3") @ mxq(f64(w_q), 0, "e4m3")) + f64(b_q)
    h = v / np.sqrt(np.mean(v * v, axis=1, keepdims=True)) * f64(gain) * f64(conf)[:, None]
    d = (mxq(f64(y), 1, "e4m3") @ mxq(f64(w_d), 0, "e4m3")) + f64(b_d)
    z = (mxq(h, 1, "e4m3") @ mxq(d, 1, "e4m3").T) * f64(inv_temp)[:, None] + f64(prior)
    e = np.exp(z - np.max(z, axis=1, keepdims=True))
    lift = e / np.mean(e, axis=1, keepdims=True)
    c = mxq(f64(clicks), 1, "e4m3") @ mxq(h, 0, "e4m3")
    docs = d * f64(keep) + c * f64(move)
    return lift, docs


def e4m3fn_bytes(y):
    return np.clip(np.asarray(y, np.float64), -448.0, 448.0).astype(np.float32).astype(ml_dtypes.float8_e4m3fn).view(np.uint8)


def e4m3fn_values(b):
    return np.asarray(b, np.uint8).view(ml_dtypes.float8_e4m3fn).astype(np.float64)


def setup_inputs():
    d = draw0()
    x0 = np.asarray(d['y']).astype(np.float64)
    s = (np.max(np.abs(x0), axis=(0,), keepdims=True) / 448.0).astype(np.float32)
    out = {}
    for k, v in d.items():
        if k == 'y':
            out['y_bytes'] = e4m3fn_bytes(x0 / s.astype(np.float64))
            out['y_scale'] = s
        else:
            out[k] = v
    return out


def reference(x, w_q, b_q, gain, conf, y_bytes, y_scale, w_d, b_d, inv_temp, prior, clicks, keep, move):
    return core(x, w_q, b_q, gain, conf, e4m3fn_values(y_bytes) * y_scale.astype(np.float64), w_d, b_d, inv_temp, prior, clicks, keep, move)

from contextlib import ExitStack

import concourse.mybir as mybir
from concourse.masks import make_identity

M, K, F, N, J = 1024, 1536, 512, 2048, 1024
BY_SCALAR = (2, 5)
FLOPS = 2 * (M * K * F + N * J * F + M * F * N + N * M * F)

P = 128
CH = 512
NC = N // CH
NG = M // CH

F32 = mybir.dt.float32
BF16 = mybir.dt.bfloat16
U8 = mybir.dt.uint8
U32 = mybir.dt.uint32
FP8 = mybir.dt.float8_e4m3fn
X4 = mybir.dt.float8_e4m3fn_x4
ACT = mybir.ActivationFunctionType
ALU = mybir.AluOpType
AX = mybir.AxisListType


def tile_retrieval_click_feedback_f6_kernel(
    tc, x, w_q, b_q, gain, conf, y_bytes, y_scale, w_d, b_d, inv_temp, prior, clicks, keep, move, lift, docs
):
    nc = tc.nc
    with ExitStack() as ctx:
        hold = ctx.enter_context(tc.tile_pool(name="hold", bufs=1))
        mid = ctx.enter_context(tc.tile_pool(name="mid", bufs=2))
        psum = ctx.enter_context(tc.psum_pool(name="psum", bufs=4))
        pool = {}

        with tc.tile_pool(name="early", bufs=2) as early:
            pool["early"] = early
            ident = hold.tile([P, P], F32, name="ident")
            make_identity(nc, ident[:])
            warm = hold.tile([P, 1], F32, name="warm")
            nc.gpsimd.memset(warm[:], 1.0)
            warm_out = hold.tile([P, 1], F32, name="warm_out")
            nc.scalar.activation(out=warm_out[:], in_=warm[:], func=ACT.Sqrt)

            scale_b = pool["early"].tile([P, J], F32, name="scale_b", bufs=1)
            nc.scalar.dma_start(out=scale_b[:], in_=y_scale.rearrange("o k -> (o k)").partition_broadcast(P))

            wd_raw, y_raw, clk_raw, wq_raw, x_raw = {}, {}, {}, {}, {}

            def load_wd(g):
                wd_raw[g] = mid.tile([P, 4, F], BF16, name=f"wd_raw{g}", tag="raw", bufs=8)
                nc.sync.dma_start(out=wd_raw[g][:], in_=w_d.rearrange("(g p j) f -> g p j f", p=P, j=4)[g])

            def load_y(c):
                y_raw[c] = pool["early"].tile([P, 4, J], U8, name=f"y_raw{c}", bufs=1)
                nc.sync.dma_start(out=y_raw[c][:], in_=y_bytes.rearrange("(c a p) j -> c p a j", p=P, a=4)[c])

            def load_clk(c, hf):
                clk_raw[c, hf] = mid.tile([P, 2, M], BF16, name=f"clk_raw{c}_{hf}", tag="raw", bufs=8)
                nc.sync.dma_start(out=clk_raw[c, hf][:], in_=clicks.rearrange("(c h a p) m -> c h p a m", p=P, a=2, h=2)[c, hf])

            def load_wq(k):
                wq_raw[k] = mid.tile([P, 4, F], BF16, name=f"wq_raw{k}", tag="raw", bufs=8)
                nc.sync.dma_start(out=wq_raw[k][:], in_=w_q.rearrange("(g p j) f -> g p j f", p=P, j=4)[k])

            def load_x(g, t):
                x_raw[g, t] = mid.tile([P, K], BF16, name=f"x_raw{g}_{t}", tag="raw", bufs=8)
                nc.sync.dma_start(out=x_raw[g, t][:], in_=x.rearrange("(g i t) k -> g t i k", i=P, t=4)[g, t])

            load_wd(0)
            load_y(0)
            load_wd(1)
            for k in range(3):
                load_wq(k)
            load_y(1)
            load_clk(0, 0)
            load_clk(0, 1)
            load_y(2)

            def column(name, src, cols):
                raw = hold.tile([P, cols], BF16, name=name + "_raw")
                with nc.allow_non_contiguous_dma(reason="a few hundred short rows"):
                    nc.scalar.dma_start(out=raw[:], in_=src)
                full = hold.tile([P, cols], F32, name=name)
                nc.gpsimd.tensor_scalar(out=full[:], in0=raw[:], scalar1=1.0, scalar2=0.0, op0=ALU.mult, op1=ALU.add)
                return full

            bd_c = column("bd_c", b_d.rearrange("(p t) -> p t", t=4), 4)
            keep_c = column("keep_c", keep.rearrange("(p t) -> p t", t=4), 4)
            move_c = column("move_c", move.rearrange("(p t) -> p t", t=4), 4)

            def column2(name, src):
                raw = hold.tile([P, NG, 4], BF16, name=name + "_raw")
                with nc.allow_non_contiguous_dma(reason="a few hundred short rows"):
                    nc.scalar.dma_start(out=raw[:], in_=src.rearrange("(g p t) -> p g t", p=P, t=4))
                full = hold.tile([P, NG, 4], F32, name=name)
                nc.gpsimd.tensor_scalar(out=full[:], in0=raw[:], scalar1=1.0, scalar2=0.0, op0=ALU.mult, op1=ALU.add)
                return full

            conf_c = column2("conf_c", conf)
            temp_c = column2("temp_c", inv_temp)

            def spread(name, src, width):
                t = hold.tile([P, width], BF16, name=name)
                nc.scalar.dma_start(out=t[:], in_=src.partition_broadcast(P))
                return t

            bq_b = spread("bq_b", b_q, F)
            gain_b = spread("gain_b", gain, F)
            prior_b = spread("prior_b", prior, N)

            wd_codes = pool["early"].tile([P, 2, F], U32, name="wd_codes", bufs=1, align_bytes=64)
            wd_sc = pool["early"].tile([P, 2, F], U8, name="wd_sc", bufs=1, align_bytes=64)
            wq_codes = hold.tile([P, 3, F], U32, name="wq_codes", align_bytes=64)
            wq_sc = hold.tile([P, 3, F], U8, name="wq_sc", align_bytes=64)
            clk_codes = hold.tile([P, NC, 2, CH], U32, name="clk_codes", align_bytes=64)
            clk_sc = hold.tile([P, NC, 2, CH], U8, name="clk_sc", align_bytes=64)
            d_codes = hold.tile([P, N], U32, name="d_codes", align_bytes=64)
            d_sc = hold.tile([P, N], U8, name="d_sc", align_bytes=64)
            hT_codes = hold.tile([P, NG, CH], U32, name="hT_codes", align_bytes=64)
            hT_sc = hold.tile([P, NG, CH], U8, name="hT_sc", align_bytes=64)
            hfb_codes = hold.tile([P, NG, F], U32, name="hfb_codes", align_bytes=64)
            hfb_sc = hold.tile([P, NG, F], U8, name="hfb_sc", align_bytes=64)
            d32 = hold.tile([P, 4, N], F32, name="d32")
            h16 = {g: hold.tile([P, 4, F], BF16, name=f"h16_{g}") for g in range(NG)}
            ss = {g: hold.tile([P, 4], F32, name=f"ss{g}") for g in range(NG)}
            rt = {g: hold.tile([P, 4], F32, name=f"rt{g}") for g in range(NG)}
            rr = {g: hold.tile([P, 4], F32, name=f"rr{g}") for g in range(NG)}
            rc = {g: hold.tile([P, 4], F32, name=f"rc{g}") for g in range(NG)}

            def turn_bank():
                return psum.tile([P, 4, P], F32, name="turned", tag="turn", bufs=4)

            def product_bank():
                return psum.tile([P, CH], F32, name="product", tag="product", bufs=4)

            def quantize(codes, scales, grouped):
                nc.vector.quantize_mx(out=codes.bitcast(X4), scales=scales, in_=grouped)

            def grouped4(name):
                return mid.tile([P, 2048], BF16, name=name, tag="grouped4", bufs=4, align_bytes=64)

            def grouped8(name):
                return pool["early"].tile([P, 2, 2048], BF16, name=name, tag="grouped8", bufs=3, align_bytes=64)

            wgrp = {}

            def wd_int(g, copy):
                if g == 0:
                    wgrp["d"] = grouped8("wd_grp")
                copy(
                    out=wgrp["d"][:, g, :].rearrange("p (t m j) -> p t m j", t=4, j=4),
                    in_=wd_raw[g][:].rearrange("p j (m t) -> p t m j", t=4),
                )

            def flat(t):
                return t[:].rearrange("p g n -> p (g n)")

            def wd_quant():
                quantize(flat(wd_codes), flat(wd_sc), flat(wgrp["d"]))

            def wq_int(k, copy):
                wgrp["q", k] = grouped4("wq_grp")
                copy(
                    out=wgrp["q", k][:].rearrange("p (f j) -> p f j", j=4),
                    in_=wq_raw[k][:].rearrange("p j f -> p f j"),
                )

            def wq_quant(k):
                quantize(wq_codes[:, k, :], wq_sc[:, k, :], wgrp["q", k][:])

            def turn_rows(rows):
                words = rows.bitcast(F32)
                bank = turn_bank()
                for g in range(2):
                    for u in range(2):
                        nc.tensor.transpose(bank[:, 2 * g + u, :], words[:, 256 * g + u : 256 * (g + 1) : 2], ident[:])
                return bank

            def empty_rows(bank, grp, a):
                words = grp[:].bitcast(F32).rearrange("p g (n u) -> p g n u", u=2)
                nc.scalar.copy(
                    out=words[:, :, P * a : P * (a + 1), :], in_=bank[:].rearrange("p (g u) n -> p g n u", g=2)
                )

            y16, ybank, ygrp, ycodes, ysc, dbank, dgrp = {}, {}, {}, {}, {}, {}, {}

            def y_mul(c, a):
                y16[c, a] = pool["early"].tile([P, J], BF16, name="y16", tag="y16", bufs=4)
                nc.vector.tensor_tensor(out=y16[c, a][:], in0=y_raw[c][:, a, :].bitcast(FP8), in1=scale_b[:], op=ALU.mult)

            def y_turn(c, a):
                ybank[c, a] = turn_rows(y16[c, a][:])

            def y_exit(c, a):
                if a == 0:
                    ygrp[c] = grouped8("ygrp")
                empty_rows(ybank[c, a], ygrp[c], a)

            def y_quant(c):
                ycodes[c] = pool["early"].tile([P, 2, CH], U32, name="ycodes", tag="ycodes", bufs=2, align_bytes=64)
                ysc[c] = pool["early"].tile([P, 2, CH], U8, name="ysc", tag="ysc", bufs=2, align_bytes=64)
                quantize(flat(ycodes[c]), flat(ysc[c]), flat(ygrp[c]))

            def d_mm(c, t):
                dbank[c, t] = product_bank()
                for g in range(2):
                    nc.tensor.matmul_mx(
                        out=dbank[c, t][:],
                        lhsT=wd_codes[:, g, P * t : P * (t + 1)].bitcast(X4),
                        lhsT_scale=wd_sc[:, g, P * t : P * (t + 1)],
                        rhs=ycodes[c][:, g, :].bitcast(X4),
                        rhs_scale=ysc[c][:, g, :],
                        start=(g == 0),
                        stop=(g == 1),
                    )

            def d_exit(c, t):
                nc.scalar.activation(
                    out=d32[:, t, CH * c : CH * (c + 1)], in_=dbank[c, t][:], func=ACT.Identity, bias=bd_c[:, t : t + 1]
                )

            def d_int(c):
                dgrp[c] = grouped4("dgrp")
                nc.vector.tensor_copy(
                    out=dgrp[c][:].rearrange("p (n t) -> p n t", t=4),
                    in_=d32[:, :, CH * c : CH * (c + 1)].rearrange("p t n -> p n t"),
                )

            def d_quant(c):
                quantize(d_codes[:, CH * c : CH * (c + 1)], d_sc[:, CH * c : CH * (c + 1)], dgrp[c][:])

            def dk(t):
                nc.gpsimd.tensor_scalar(
                    out=d32[:, t, :], in0=d32[:, t, :], scalar1=keep_c[:, t : t + 1], scalar2=1.0, op0=ALU.mult, op1=ALU.mult
                )

            cbank, cgrp = {}, {}

            def clk_turn(c, a):
                cbank[c, a] = turn_rows(clk_raw[c, a // 2][:, a % 2, :])

            def clk_exit(c, a):
                if a == 0:
                    cgrp[c] = grouped8("cgrp")
                empty_rows(cbank[c, a], cgrp[c], a)

            def clk_quant(c):
                quantize(
                    clk_codes[:, c].rearrange("p g n -> p (g n)"), clk_sc[:, c].rearrange("p g n -> p (g n)"), flat(cgrp[c])
                )

            xbank, xgrp, xcodes, xsc, vbank, v32, hbank, hgrp, fgrp = {}, {}, {}, {}, {}, {}, {}, {}, {}

            def x_turn(g, k, pr):
                bank = turn_bank()
                for b in range(2):
                    words = x_raw[g, 2 * pr + b][:].bitcast(F32)
                    for u in range(2):
                        nc.tensor.transpose(bank[:, 2 * b + u, :], words[:, 256 * k + u : 256 * (k + 1) : 2], ident[:])
                xbank[g, k, pr] = bank

            def x_exit(g, k, pr):
                if pr == 0:
                    xgrp[g, k] = grouped4("xgrp")
                words = xgrp[g, k][:].bitcast(F32).rearrange("p (b n u) -> p b n u", u=2, b=4)
                nc.scalar.copy(
                    out=words[:, 2 * pr : 2 * pr + 2, :, :], in_=xbank[g, k, pr][:].rearrange("p (b u) n -> p b n u", b=2)
                )

            def x_quant(g, k):
                if k == 0:
                    xcodes[g] = mid.tile([P, 3, CH], U32, name="xcodes", tag="xcodes", bufs=2, align_bytes=64)
                    xsc[g] = mid.tile([P, 3, CH], U8, name="xsc", tag="xsc", bufs=2, align_bytes=64)
                quantize(xcodes[g][:, k, :], xsc[g][:, k, :], xgrp[g, k][:])

            def v_mm(g, t):
                vbank[g, t] = product_bank()
                for k in range(3):
                    nc.tensor.matmul_mx(
                        out=vbank[g, t][:],
                        lhsT=xcodes[g][:, k, P * t : P * (t + 1)].bitcast(X4),
                        lhsT_scale=xsc[g][:, k, P * t : P * (t + 1)],
                        rhs=wq_codes[:, k, :].bitcast(X4),
                        rhs_scale=wq_sc[:, k, :],
                        start=(k == 0),
                        stop=(k == 2),
                    )

            def v_add(g, t):
                v32[g, t] = mid.tile([P, F], F32, name="v32", tag="v32", bufs=5)
                nc.vector.tensor_tensor(out=v32[g, t][:], in0=vbank[g, t][:], in1=bq_b[:], op=ALU.add)

            def v_sq(g, t):
                junk = mid.tile([P, F], BF16, name="junk", tag="junk", bufs=2)
                nc.scalar.activation(out=junk[:], in_=v32[g, t][:], func=ACT.Square, accum_out=ss[g][:, t : t + 1])

            def h_root(g):
                nc.scalar.activation(out=rt[g][:], in_=ss[g][:], func=ACT.Sqrt, scale=1.0 / F)

            def h_rec(g):
                nc.vector.reciprocal(out=rr[g][:], in_=rt[g][:])

            def h_conf(g):
                nc.vector.tensor_tensor(out=rc[g][:], in0=rr[g][:], in1=conf_c[:, g, :], op=ALU.mult)

            def h_mul(g, t):
                nc.vector.scalar_tensor_tensor(
                    out=h16[g][:, t, :], in0=v32[g, t][:], scalar=rc[g][:, t : t + 1], in1=gain_b[:], op0=ALU.mult, op1=ALU.mult
                )

            def h_turn(g, pr):
                bank = turn_bank()
                for b in range(2):
                    words = h16[g][:, 2 * pr + b, :].bitcast(F32)
                    for u in range(2):
                        nc.tensor.transpose(bank[:, 2 * b + u, :], words[:, u : 256 : 2], ident[:])
                hbank[g, pr] = bank

            def h_exit(g, pr):
                if pr == 0:
                    hgrp[g] = grouped4("hgrp")
                words = hgrp[g][:].bitcast(F32).rearrange("p (b n u) -> p b n u", u=2, b=4)
                nc.scalar.copy(
                    out=words[:, 2 * pr : 2 * pr + 2, :, :], in_=hbank[g, pr][:].rearrange("p (b u) n -> p b n u", b=2)
                )

            def hT_quant(g):
                quantize(hT_codes[:, g, :], hT_sc[:, g, :], hgrp[g][:])

            def hfb_int(g):
                fgrp[g] = grouped4("fgrp")
                for t in range(4):
                    nc.gpsimd.tensor_scalar(
                        out=fgrp[g][:, CH * t : CH * (t + 1)].rearrange("p (i r) -> p i r", r=4),
                        in0=h16[g][:].rearrange("p r (i t) -> p t i r", t=4)[:, t],
                        scalar1=1.0,
                        scalar2=0.0,
                        op0=ALU.mult,
                        op1=ALU.add,
                    )

            def hfb_quant(g):
                quantize(hfb_codes[:, g, :], hfb_sc[:, g, :], fgrp[g][:])

            zbank, z, top, total, share, out_t = {}, {}, {}, {}, {}, {}

            def z_mm(i, c):
                g, t = divmod(i, 4)
                zbank[i, c] = product_bank()
                nc.tensor.matmul_mx(
                    out=zbank[i, c][:],
                    lhsT=hT_codes[:, g, P * t : P * (t + 1)].bitcast(X4),
                    lhsT_scale=hT_sc[:, g, P * t : P * (t + 1)],
                    rhs=d_codes[:, CH * c : CH * (c + 1)].bitcast(X4),
                    rhs_scale=d_sc[:, CH * c : CH * (c + 1)],
                    start=True,
                    stop=True,
                )

            def z_add(i, c):
                g, t = divmod(i, 4)
                if c == 0:
                    z[i] = pool["late"].tile([P, N], F32, name="z", tag="z", bufs=3)
                    top[i] = pool["late"].tile([P, 1], F32, name="top", tag="top", bufs=3)
                    total[i] = pool["late"].tile([P, 1], F32, name="total", tag="total", bufs=3)
                    share[i] = pool["late"].tile([P, 1], F32, name="share", tag="share", bufs=3)
                cols = slice(CH * c, CH * (c + 1))
                if i in BY_SCALAR:
                    nc.scalar.activation(out=z[i][:, cols], in_=zbank[i, c][:], func=ACT.Copy, scale=temp_c[:, g, t : t + 1])
                    nc.gpsimd.tensor_tensor(out=z[i][:, cols], in0=z[i][:, cols], in1=prior_b[:, cols], op=ALU.add)
                    return
                nc.vector.scalar_tensor_tensor(
                    out=z[i][:, cols], in0=zbank[i, c][:], scalar=temp_c[:, g, t : t + 1], in1=prior_b[:, cols], op0=ALU.mult, op1=ALU.add
                )

            def z_max(i):
                nc.vector.tensor_reduce(out=top[i][:], in_=z[i][:], axis=AX.X, op=ALU.max, negate=True)

            def z_exp(i):
                nc.scalar.activation(out=z[i][:], in_=z[i][:], func=ACT.Exp, bias=top[i][:], scale=1.0, accum_out=total[i][:])

            def z_rec(i):
                nc.vector.reciprocal(out=share[i][:], in_=total[i][:])

            def z_mul(i):
                out_t[i] = pool["late"].tile([P, N], F32, name="out_t", tag="out_t", bufs=2)
                if i == 7:
                    for eng, c0, c1 in ((nc.vector, 0, 1024), (nc.gpsimd, 1024, 1536)):
                        eng.tensor_scalar(
                            out=out_t[i][:, c0:c1], in0=z[i][:, c0:c1], scalar1=share[i][:], scalar2=float(N), op0=ALU.mult, op1=ALU.mult
                        )
                    half = pool["late"].tile([P, 1], F32, name="half", bufs=1)
                    nc.vector.tensor_scalar(out=half[:], in0=share[i][:], scalar1=float(N), scalar2=None, op0=ALU.mult)
                    nc.scalar.activation(out=out_t[i][:, 1536:], in_=z[i][:, 1536:], func=ACT.Copy, scale=half[:])
                    return
                nc.gpsimd.tensor_scalar(
                    out=out_t[i][:], in0=z[i][:], scalar1=share[i][:], scalar2=float(N), op0=ALU.mult, op1=ALU.mult
                )

            def z_store(i):
                g, t = divmod(i, 4)
                rows = lift.rearrange("(g i t) n -> g t i n", i=P, t=4)[g, t]
                for c0, c1 in ((0, N),) if i < 7 else ((0, 1024), (1024, 1536), (1536, N)):
                    nc.sync.dma_start(out=rows[:, c0:c1], in_=out_t[i][:, c0:c1])

            fbank, cm, docbank = {}, {}, {}

            def c_mm(c, t):
                bank = psum.tile([P, CH], F32, name="feedback", tag="turn", bufs=4)
                fbank[c, t] = bank
                for g in range(2):
                    nc.tensor.matmul_mx(
                        out=bank[:],
                        lhsT=hfb_codes[:, g, P * t : P * (t + 1)].bitcast(X4),
                        lhsT_scale=hfb_sc[:, g, P * t : P * (t + 1)],
                        rhs=clk_codes[:, c, g, :].bitcast(X4),
                        rhs_scale=clk_sc[:, c, g, :],
                        start=(g == 0),
                        stop=(g == 1),
                    )

            def c_exit(c, t):
                if t == 0:
                    cm[c] = pool["late"].tile([P, 4, CH], F32, name="cm", tag="cm", bufs=2)
                nc.scalar.activation(out=cm[c][:, t, :], in_=fbank[c, t][:], func=ACT.Copy, scale=move_c[:, t : t + 1])

            def doc_turn(c, a):
                bank = turn_bank()
                for t in range(4):
                    nc.tensor.matmul(
                        bank[:, t, :], lhsT=d32[:, t, CH * c + P * a : CH * c + P * (a + 1)], rhs=ident[:], start=True, stop=False, is_transpose=True
                    )
                    nc.tensor.matmul(
                        bank[:, t, :], lhsT=cm[c][:, t, P * a : P * (a + 1)], rhs=ident[:], start=False, stop=True, is_transpose=True
                    )
                docbank[c, a] = bank

            def doc_exit(c, a):
                o = pool["late"].tile([P, F], F32, name="doc_o", tag="doc_o", bufs=3)
                nc.scalar.copy(out=o[:].rearrange("p (i t) -> p i t", t=4), in_=docbank[c, a][:].rearrange("p t i -> p i t"))
                nc.sync.dma_start(out=docs.rearrange("(c a p) f -> c a p f", p=P, a=4)[c, a], in_=o[:])

            def late_loads():
                load_clk(1, 0)
                load_clk(1, 1)
                load_y(3)
                for t in range(4):
                    load_x(0, t)
                load_clk(2, 0)
                load_clk(2, 1)
                for t in range(4):
                    load_x(1, t)
                load_clk(3, 0)
                load_clk(3, 1)

            late_loads()
            wd_int(0, nc.scalar.copy)
            wd_int(1, nc.scalar.copy)
            wd_quant()

            fill = {
                0: [lambda: wq_int(0, nc.vector.tensor_copy), lambda: wq_int(1, nc.vector.tensor_copy), lambda: wq_int(2, nc.vector.tensor_copy), lambda: wq_quant(0)],
                1: [lambda: wq_quant(1), lambda: wq_quant(2), lambda: None, lambda: None],
                2: [lambda: None, lambda: None, lambda: clk_quant(0), lambda: None],
                3: [lambda: None, lambda: None, lambda: clk_quant(1), lambda: None],
            }
            xt = [(g, k, pr) for g in range(NG) for k in range(3) for pr in range(2)]

            def turn_x(n):
                for e in xt[:n]:
                    x_turn(*e)
                    x_exit(*e)
                del_n = xt[n:]
                xt.clear()
                xt.extend(del_n)

            for c in range(NC):
                for a in range(4):
                    y_mul(c, a)
                    fill[c][a]()
                    y_turn(c, a)
                    y_exit(c, a)
                    if c >= 1:
                        if a == 0 and c >= 2:
                            d_int(c - 2)
                            d_quant(c - 2)
                        if a == 1:
                            y_quant(c - 1)
                            for t in range(4):
                                d_mm(c - 1, t)
                        if a >= 2:
                            d_exit(c - 1, 2 * a - 4)
                            d_exit(c - 1, 2 * a - 3)
                        clk_turn(c - 1, a)
                        clk_exit(c - 1, a)
            d_int(2)
            d_quant(2)
            clk_quant(2)
            turn_x(4)
            y_quant(3)
            for t in range(4):
                d_mm(3, t)
            turn_x(2)
            for k in range(3):
                x_quant(0, k)
            for t in range(4):
                d_exit(3, t)
            for t in range(4):
                v_mm(0, t)
                v_add(0, t)
                v_sq(0, t)
            turn_x(6)
            d_int(3)
            d_quant(3)
            for t in range(4):
                dk(t)
            h_root(0)
            h_rec(0)
            h_conf(0)
            for k in range(3):
                x_quant(1, k)
            for t in range(4):
                h_mul(0, t)
                if t % 2:
                    h_turn(0, t // 2)
                    h_exit(0, t // 2)
            for t in range(4):
                v_mm(1, t)
                v_add(1, t)
                v_sq(1, t)
            hT_quant(0)
            hfb_int(0)
            h_root(1)
            for a in range(4):
                clk_turn(3, a)
                clk_exit(3, a)
            h_rec(1)
            h_conf(1)
            hfb_quant(0)
            for t in range(4):
                h_mul(1, t)
                if t % 2:
                    h_turn(1, t // 2)
                    h_exit(1, t // 2)
            for c in range(4):
                z_mm(0, c)
            hT_quant(1)
            hfb_int(1)
            clk_quant(3)
            hfb_quant(1)
        with tc.tile_pool(name="late", bufs=2) as late:
            pool["late"] = late

            work = []
            for c in range(5):
                for t in range(4):
                    if c < 4:
                        work.append((c_mm, c_exit, c, t))
                    if c >= 1:
                        work.append((doc_turn, doc_exit, c - 1, t))

            def feed(n):
                for e in work[:n]:
                    e[0](e[2], e[3])
                    e[1](e[2], e[3])
                rest = work[n:]
                work.clear()
                work.extend(rest)

            for i in range(9):
                if i < 8:
                    for c in range(4):
                        z_add(i, c)
                        if i + 1 < 8:
                            z_mm(i + 1, c)
                    if i >= 1:
                        z_rec(i - 1)
                    z_max(i)
                feed(4)
                if i < 8:
                    z_exp(i)
                if i == 8:
                    z_rec(i - 1)
                if i >= 1:
                    z_mul(i - 1)
                    z_store(i - 1)
            feed(99)
